import numpy as np
import ml_dtypes


def mxq(x, axis, fmt="e4m3"):
    dtype, down = {"e4m3": (ml_dtypes.float8_e4m3fn, 7), "e5m2": (ml_dtypes.float8_e5m2, 14)}[fmt]
    v = np.moveaxis(np.asarray(x, np.float32).astype(ml_dtypes.bfloat16).astype(np.float64), axis, -1)
    blocks = v.reshape(v.shape[:-1] + (-1, 32))
    amax = np.abs(blocks).max(-1, keepdims=True)
    byte = np.maximum(np.where(amax > 0, np.frexp(amax)[1] - 1 + 127, 0) - down, 1)
    scale = np.exp2(byte - 127.0)
    codes = (blocks / scale).astype(np.float32).astype(dtype).astype(np.float64)
    return np.moveaxis((codes * scale).reshape(v.shape), -1, axis)


WIDE = False


def mx_kscale(k):
    if not WIDE:
        return np.ones(k)
    levels = np.array([10, -10, 5, -5, 0])
    if k % 512:
        return np.exp2(np.random.permutation(np.resize(levels, k // 32))).repeat(32)
    a = np.empty((k // 512, 16))
    for p in range(k // 512):
        a[p, :8] = np.random.permutation(np.resize(levels, 8))
        for g in range(8):
            far = levels[np.abs(levels - a[p, g]) >= 10]
            a[p, g + 8] = far[np.random.randint(len(far))]
    return np.exp2(a.ravel()).repeat(32)


def f64(x):
    return np.asarray(x).astype(np.float64)


def striped(idx):
    return np.tile(idx.reshape(-1, 16).T, (8, 1)).astype(np.uint16)


def unstriped(offs):
    return offs[:16].T.reshape(-1).astype(np.int64)


E2M1 = np.array([0.0, 0.5, 1.0, 1.5, 2.0, 3.0, 4.0, 6.0, -0.0, -0.5, -1.0, -1.5, -2.0, -3.0, -4.0, -6.0])


def pack_weight(w, fmt):
    k, n = w.shape
    w = f64(np.asarray(w, np.float32).astype(ml_dtypes.bfloat16)).reshape(k // 32, 32, n)
    amax = np.abs(w).max(1)
    if fmt == "e4m3":
        byte = np.frexp(amax)[1] - 1 + 127 - 7
    else:
        mant, ex = np.frexp(amax / 6.0)
        byte = np.where(mant > 0.5, ex, ex - 1) + 127
    byte = np.clip(np.where(amax > 0, byte, 1), 1, 254)
    scaled = (w * np.exp2(127.0 - byte)[:, None, :]).reshape(k, n).astype(np.float32)
    by_word = np.ascontiguousarray(scaled.reshape(k // 512, 128, 4, n).transpose(0, 1, 3, 2))
    if fmt == "e4m3":
        words = by_word.astype(ml_dtypes.float8_e4m3fn).view(np.uint8)
    else:
        c = by_word.astype(ml_dtypes.float4_e2m1fn).view(np.uint8) & 0xF
        words = (c[..., 0::2] | (c[..., 1::2] << 4)).reshape(k // 512, 128, 2 * n)
    return np.ascontiguousarray(words), np.ascontiguousarray(byte.astype(np.uint8).reshape(k // 512, 16, n))


def unpack_weight(words, scales, fmt):
    g, _, n = scales.shape
    words = np.ascontiguousarray(words).reshape(g, 128, n, -1)
    if fmt == "e4m3":
        vals = words.view(ml_dtypes.float8_e4m3fn).astype(np.float64)
    else:
        nib = np.empty((g, 128, n, 4), np.uint8)
        nib[..., 0::2] = words & 0xF
        nib[..., 1::2] = words >> 4
        vals = E2M1[nib]
    vals = vals * np.repeat(np.exp2(scales.astype(np.float64) - 127.0), 8, axis=1)[..., None]
    return vals.transpose(0, 1, 3, 2).reshape(g * 512, n)


def gelu(v):
    return 0.5 * v * (1.0 + np.tanh(np.sqrt(2.0 / np.pi) * (v + 0.044715 * v**3)))


def striped8(idx):
    return np.concatenate([v.reshape(-1, 16).T for v in idx]).astype(np.uint16)


def unstriped8(offs):
    return np.stack([offs[16 * g:16 * g + 16].T.reshape(-1) for g in range(8)]).astype(np.int64)


def heads(h, wgt, idx8):
    r = np.arange(h.shape[0])
    return wgt[r // 4 % 128] * h[r[:, None], idx8[r % 512 // 64]]


def put_heads(h, wgs, idx8, t2):
    r = np.arange(h.shape[0])
    page = np.zeros((h.shape[0], t2))
    page[r[:, None], idx8[r % 512 // 64]] = wgs[r // 4 % 128] * h
    return page


K, H, N, T, S, P, T2 = 1024, 1024, 512, 4096, 1024, 1024, 2048

def setup_inputs():
    n = np.random.standard_normal
    s = mx_kscale(K)[:, None]
    u = mx_kscale(H)[:, None]
    d = {}
    d["tab_words"], d["tab_scales"] = pack_weight(n((K, T)) * s, "e4m3")
    d["offs"] = striped(np.random.permutation(T)[:S])
    d["offs2"] = striped8(np.stack([np.random.permutation(T2)[:S] for _ in range(8)]))
    d["offs3"] = striped8(np.stack([np.random.permutation(T2)[:P] for _ in range(8)]))
    d["w1"] = (1.5 * n((K, H)) / s / K ** 0.5).astype(np.float32)
    d["b1"] = (0.6 * n(H)).astype(np.float32)
    d["gain"] = (u[:, 0] * np.exp(0.3 * n(H))).astype(np.float32)
    d["wgs"] = np.repeat(np.random.uniform(0.5, 2.0, (8, S)), 16, axis=0).astype(np.float32)
    d["wgt"] = np.repeat(np.random.uniform(0.5, 2.0, (8, P)), 16, axis=0).astype(np.float32)
    d["tempo"] = (0.8 * n((H, P)) * u).astype(np.float32)
    d["w4_words"], d["w4_scales"] = pack_weight(n((H, N)) / u / H ** 0.5, "e2m1")
    d["w5"] = (1.3 * n((H, N)) / u / H ** 0.5).astype(np.float32)
    d["b2"] = (0.6 * n(N)).astype(np.float32)
    return d

def reference(tab_words, tab_scales, offs, offs2, offs3, w1, b1, gain, wgs, wgt, tempo, w4_words, w4_scales, w5, b2):
    v = unpack_weight(tab_words, tab_scales, "e4m3")[:, unstriped(offs)]
    e = (mxq(f64(w1), 0, "e4m3").T @ v) + f64(b1)[:, None]
    h = f64(gain)[:, None] * np.tanh(e)
    page = put_heads(h, f64(wgs), unstriped8(offs2), T2)
    x = heads(page, f64(wgt), unstriped8(offs3))
    z = x - f64(tempo)
    zq = mxq(z, 0, "e4m3")
    hq = mxq(h, 0, "e4m3")
    w4 = unpack_weight(w4_words, w4_scales, "e2m1")
    y = w4.T @ zq + mxq(f64(w5), 0, "e4m3").T @ hq
    return y + f64(b2)[:, None]

@@ -1,0 +1,329 @@
+from contextlib import ExitStack
+
+import concourse.mybir as mybir
+from concourse.masks import make_identity
+
+K, H, N, T, S, T2 = 1024, 1024, 512, 4096, 1024, 2048
+FLOPS = 2 * K * H * S + 2 * 2 * H * N * S
+
+F32 = mybir.dt.float32
+BF16 = mybir.dt.bfloat16
+I32 = mybir.dt.int32
+U32 = mybir.dt.uint32
+U16 = mybir.dt.uint16
+U8 = mybir.dt.uint8
+FP8X4 = mybir.dt.float8_e4m3fn_x4
+FP4X4 = mybir.dt.float4_e2m1fn_x4
+ALU = mybir.AluOpType
+ACT = mybir.ActivationFunctionType
+
+P = 128
+PACK = 4
+PASS = P * PACK
+HALF = 512
+CHUNKS = [(0, 256), (256, 256), (512, 256), (768, 128), (896, 128)]
+PER_COL = 16
+
+
+def tile_list_fencing_bout_replay_kernel(
+    tc, tab_words, tab_scales, offs, offs2, offs3, w1, b1, gain, wgs, wgt, tempo, w4_words, w4_scales, w5, b2, out
+):
+    nc = tc.nc
+    with ExitStack() as ctx:
+        keep = ctx.enter_context(tc.tile_pool(name="keep", bufs=1))
+        ring = ctx.enter_context(tc.tile_pool(name="ring", bufs=2))
+        psum = ctx.enter_context(tc.psum_pool(name="psum", bufs=1))
+
+        def entries(list_tile, start, count):
+            return list_tile[:, start // PER_COL : (start + count) // PER_COL]
+
+        banks = [psum.tile([P, 512], F32, name="bank%d" % n) for n in range(8)]
+
+        pick = keep.tile([P, S // PER_COL], U16, name="pick")
+        nc.sync.dma_start(pick[:], offs)
+
+        def load_table(a):
+            words = keep.tile([P, T], I32, name="table%d" % a, tag="slab%d" % a, align_bytes=64)
+            nc.sync.dma_start(words[:], tab_words[a].rearrange("p t i -> p (t i)").bitcast(I32))
+            return words
+
+        def load_weight(src, a, col0):
+            raw = ring.tile([P, PACK, PASS], F32, name="raw", tag="raw", bufs=3)
+            nc.sync.dma_start(
+                raw[:], src[PASS * a : PASS * (a + 1), col0 : col0 + PASS].rearrange("(p j) c -> p j c", j=PACK)
+            )
+            return raw
+
+        table_plane = keep.tile([P, T], U8, name="table_plane", align_bytes=64)
+        nc.vector.memset(table_plane[:].bitcast(I32), 0)
+        table = [load_table(0)]
+
+        def load_table_scales(a):
+            for r in range(4):
+                nc.sync.dma_start(
+                    table_plane[4 * a + r : P : 32, :].bitcast(I32), tab_scales[a, r:16:4, :].bitcast(I32)
+                )
+
+        load_table_scales(0)
+        w1_raw = {}
+        w1_raw[0, 0] = load_weight(w1, 0, 0)
+        w1_raw[1, 0] = load_weight(w1, 1, 0)
+        load_table_scales(1)
+        table.append(load_table(1))
+        b1_sb = keep.tile([P, 2, PACK], F32, name="b1_sb")
+        nc.sync.dma_start(b1_sb[:], b1.rearrange("(b p i) -> p b i", b=2, i=PACK))
+        gain_sb = keep.tile([P, 2, PACK], F32, name="gain_sb")
+        nc.sync.dma_start(gain_sb[:], gain.rearrange("(b p i) -> p b i", b=2, i=PACK))
+        put = keep.tile([P, S // PER_COL], U16, name="put")
+        nc.sync.dma_start(put[:], offs2)
+        wgs_sb = keep.tile([P, S], F32, name="wgs_sb")
+        nc.sync.dma_start(wgs_sb[:], wgs)
+        read = keep.tile([P, S // PER_COL], U16, name="read")
+        nc.sync.dma_start(read[:], offs3)
+        wgt_sb = keep.tile([P, S], F32, name="wgt_sb")
+        nc.sync.dma_start(wgt_sb[:], wgt)
+
+        pages = [keep.tile([P, T2], F32, name="page%d" % n) for n in range(2)]
+        for page in pages:
+            nc.vector.memset(page[:], 0.0)
+        w4_plane = keep.tile([P, 2, N], U8, name="w4_plane", align_bytes=64)
+        nc.vector.memset(w4_plane[:].rearrange("p a n -> p (a n)").bitcast(I32), 0)
+        ident = keep.tile([P, P], F32, name="ident")
+        make_identity(nc, ident[:])
+
+        def quantize(grouped, name):
+            width = grouped.shape[1] // PACK
+            codes = keep.tile([P, width], U32, name=name + "_codes", align_bytes=64)
+            plane = keep.tile([P, width], U8, name=name + "_plane", align_bytes=64)
+            nc.vector.quantize_mx(out=codes[:].bitcast(FP8X4), scales=plane[:], in_=grouped)
+            return codes, plane
+
+        def quantize_w1(a, b):
+            grouped = ring.tile([P, PASS * PACK], BF16, name="w_bf", tag="w_bf", align_bytes=64)
+            nc.scalar.copy(
+                grouped[:].rearrange("p (t m j) -> p m t j", t=PACK, j=PACK),
+                w1_raw[a, b][:].rearrange("p j (m t) -> p m t j", t=PACK),
+            )
+            return quantize(grouped[:], "w1_%d%d" % (a, b))
+
+        def quantize_rows(src, tag, name):
+            grouped = ring.tile([P, HALF * PACK], BF16, name=tag, tag=tag, align_bytes=64)
+            nc.scalar.copy(
+                grouped[:].rearrange("p (c i j) -> p c j i", i=4, j=PACK),
+                src.rearrange("p j (c i) -> p c j i", i=4),
+            )
+            return quantize(grouped[:], name)
+
+        picked = {}
+
+        def pick_words(a, half):
+            tile = keep.tile([P, HALF], U32, name="picked%d%d" % (a, half), align_bytes=64)
+            nc.vector.tensor_copy(tile[:], table[a][:].bitcast(U32).indirect(entries(pick, HALF * half, HALF)))
+            picked[a, half] = tile
+
+        pick_words(0, 0)
+        pick_words(0, 1)
+        picked_plane = keep.tile([P, S], U8, name="picked_plane", align_bytes=64)
+        nc.vector.tensor_copy(picked_plane[:], table_plane[:].indirect(pick[:]))
+        w1q = {}
+        w1q[0, 0] = quantize_w1(0, 0)
+        w1q[1, 0] = quantize_w1(1, 0)
+        pick_words(1, 0)
+        pick_words(1, 1)
+
+        w1_raw[0, 1] = load_weight(w1, 0, PASS)
+        w1_raw[1, 1] = load_weight(w1, 1, PASS)
+
+        def load_tempo(b):
+            tile = keep.tile([P, PACK, S], F32, name="tempo%d" % b, tag="slab%d" % b, align_bytes=64)
+            nc.sync.dma_start(tile[:], tempo[PASS * b : PASS * (b + 1), :].rearrange("(p i) j -> p i j", i=PACK))
+            return tile
+
+        tempo_sb = [load_tempo(0)]
+        w5_raw = [load_weight(w5, a, 0) for a in range(2)]
+        w4_sb = keep.tile([P, 2, 2 * N], U8, name="w4_sb", align_bytes=64)
+        nc.sync.dma_start(
+            w4_sb[:].bitcast(I32), w4_words.rearrange("a p c -> p a c").bitcast(I32)
+        )
+        for r in range(4):
+            nc.sync.dma_start(
+                w4_plane[r:P:32, :, :].bitcast(I32), w4_scales[:, r:16:4, :].rearrange("a q c -> q a c").bitcast(I32)
+            )
+        tempo_sb.append(load_tempo(1))
+        b2_sb = keep.tile([P, N // P], F32, name="b2_sb")
+        with nc.allow_non_contiguous_dma(reason="one bias value a partition"):
+            nc.sync.dma_start(b2_sb[:], b2.rearrange("(t p) -> p t", p=P))
+
+        h = [keep.tile([P, PACK, S], F32, name="h%d" % b) for b in range(2)]
+
+        def make_h(s):
+            b, i = divmod(s, PACK)
+            for half in range(2):
+                bank = banks[2 * (s % 2) + half]
+                cols = slice(HALF * half, HALF * (half + 1))
+                for a in range(2):
+                    codes, plane = w1q[a, b]
+                    nc.tensor.matmul_mx(
+                        out=bank[:],
+                        lhsT=codes[:, P * i : P * (i + 1)].bitcast(FP8X4),
+                        lhsT_scale=plane[:, P * i : P * (i + 1)],
+                        rhs=picked[a, half][:].bitcast(FP8X4),
+                        rhs_scale=picked_plane[4 * a : P, cols],
+                        start=(a == 0),
+                        stop=(a == 1),
+                    )
+                nc.scalar.activation(h[b][:, i, cols], bank[:], ACT.Tanh, bias=b1_sb[:, b, i : i + 1])
+                nc.scalar.activation(h[b][:, i, cols], h[b][:, i, cols], ACT.Copy, scale=gain_sb[:, b, i : i + 1])
+
+        def place(s, pieces):
+            b, i = divmod(s, PACK)
+            width = S // pieces
+            for n in range(pieces):
+                cols = slice(width * n, width * (n + 1))
+                nc.vector.tensor_tensor(
+                    pages[s % 2][:].indirect(entries(put, width * n, width)), h[b][:, i, cols], wgs_sb[:, cols], ALU.mult
+                )
+
+        neg_x = {}
+
+        def fetch_negated(s):
+            pair, e = divmod(s, 2)
+            if e == 0:
+                neg_x[pair] = ring.tile([P, 2, S], F32, name="neg_x", tag="x", bufs=1)
+            nc.vector.tensor_tensor(neg_x[pair][:, e, :], pages[s % 2][:].indirect(read[:]), neg_wgt[:], ALU.mult)
+
+        z_bf = [
+            [keep.tile([P, HALF, PACK], BF16, name="z0_%d" % n, align_bytes=64) for n in range(2)],
+            [keep.tile([P, width, PACK], BF16, name="z1_%d" % j0, align_bytes=64) for j0, width in CHUNKS],
+        ]
+        z_cols = [[(0, HALF), (HALF, HALF)], CHUNKS
+        ]
+
+        def subtract_on_tensor(pair):
+            b, u = divmod(pair, 2)
+            for half in range(2):
+                back = banks[6 + half]
+                for g in range(2):
+                    bank = banks[4 + g]
+                    steps = [(src, jb, e) for src in range(2) for jb in range(2) for e in range(2)]
+                    for n, (src, jb, e) in enumerate(steps):
+                        j0 = HALF * half + P * (2 * g + jb)
+                        rows = tempo_sb[b][:, 2 * u + e, j0 : j0 + P] if src == 0 else neg_x[pair][:, e, j0 : j0 + P]
+                        nc.tensor.matmul(
+                            bank[:, P * (2 * jb + e) : P * (2 * jb + e + 1)],
+                            lhsT=rows,
+                            rhs=ident[:],
+                            is_transpose=True,
+                            start=(n == 0),
+                            stop=(n == len(steps) - 1),
+                        )
+                    z_t = ring.tile([P, 2, P, 2], BF16, name="z_t", tag="z_t", bufs=4)
+                    nc.scalar.activation(
+                        z_t[:], bank[:].rearrange("j (jb e p) -> j jb p e", jb=2, e=2), ACT.Copy, scale=-1.0
+                    )
+                    words = z_t[:].rearrange("j jb p e -> j jb (p e)").bitcast(F32)
+                    for jb in range(2):
+                        nc.tensor.transpose(back[:, P * (2 * g + jb) : P * (2 * g + jb + 1)], words[:, jb, :], ident[:])
+                for tile, (j0, width) in zip(z_bf[b], z_cols[b]):
+                    if j0 // HALF == half:
+                        nc.scalar.copy(tile[:].bitcast(F32)[:, :, u], back[:, j0 % HALF : j0 % HALF + width])
+
+        def quantize_h(b):
+            return [quantize_rows(h[b][:, :, HALF * n : HALF * (n + 1)], "h_bf", "h%d_%d" % (b, n)) for n in range(2)]
+
+        make_h(0)
+        place(0, 2)
+        make_h(1)
+        place(1, 1)
+        neg_wgt = keep.tile([P, S], F32, name="neg_wgt")
+        nc.scalar.activation(neg_wgt[:], wgt_sb[:], ACT.Copy, scale=-1.0)
+        fetch_negated(0)
+        fetch_negated(1)
+        w1q[0, 1] = quantize_w1(0, 1)
+        w1q[1, 1] = quantize_w1(1, 1)
+        for s in (2, 3):
+            make_h(s)
+            place(s, 1)
+        subtract_on_tensor(0)
+        fetch_negated(2)
+        fetch_negated(3)
+        hq = [quantize_h(0)]
+        for s in (4, 5):
+            make_h(s)
+            place(s, 1)
+        w5q = [quantize_rows(w5_raw[a][:], "w_bf", "w5_%d" % a) for a in range(2)]
+        subtract_on_tensor(1)
+        fetch_negated(4)
+        fetch_negated(5)
+        zq0 = [quantize(z_bf[0][n][:].rearrange("p j i -> p (j i)"), "z0q_%d" % n) for n in range(2)]
+        for s in (6, 7):
+            make_h(s)
+            place(s, 1)
+        hq.append(quantize_h(1))
+        subtract_on_tensor(2)
+
+        first_bank = [sum(width for j0, width in CHUNKS[:c]) * (N // P) // 512 for c in range(len(CHUNKS))]
+
+        def acc(c, nt):
+            width = CHUNKS[c][1]
+            bank, slot = divmod(nt, 512 // width)
+            return banks[first_bank[c] + bank][:, width * slot : width * (slot + 1)], slot
+
+        def w5_passes(b, c):
+            j0, width = CHUNKS[c]
+            codes, plane = hq[b][j0 // HALF]
+            cols = slice(j0 % HALF, j0 % HALF + width)
+            for nt in range(N // P):
+                dst, slot = acc(c, nt)
+                nc.tensor.matmul_mx(
+                    out=dst,
+                    lhsT=w5q[b][0][:, P * nt : P * (nt + 1)].bitcast(FP8X4),
+                    lhsT_scale=w5q[b][1][:, P * nt : P * (nt + 1)],
+                    rhs=codes[:, cols].bitcast(FP8X4),
+                    rhs_scale=plane[:, cols],
+                    start=(b == 0 and slot == 0),
+                    stop=False,
+                )
+
+        def w4_passes(b, c, zq, col0):
+            width = CHUNKS[c][1]
+            codes, plane = zq
+            for nt in range(N // P):
+                dst, slot = acc(c, nt)
+                for n in range(width // P):
+                    cols = slice(col0 + P * n, col0 + P * (n + 1))
+                    nc.tensor.matmul_mx(
+                        out=dst[:, P * n : P * (n + 1)],
+                        lhsT=w4_sb[:, b, 2 * P * nt : 2 * P * (nt + 1)].bitcast(FP4X4),
+                        lhsT_scale=w4_plane[:, b, P * nt : P * (nt + 1)],
+                        rhs=codes[:, cols].bitcast(FP8X4),
+                        rhs_scale=plane[:, cols],
+                        start=False,
+                        stop=(b == 1 and slot == 512 // width - 1 and n == width // P - 1),
+                    )
+
+        for c, (j0, width) in enumerate(CHUNKS):
+            w5_passes(0, c)
+            w4_passes(0, c, zq0[j0 // HALF], j0 % HALF)
+
+        out_v = out.rearrange("(t p) j -> p t j", p=P)
+        x = ring.tile([P, 2, S], F32, name="x_tail", tag="x", bufs=1)
+        for c, (j0, width) in enumerate(CHUNKS):
+            cols = slice(j0, j0 + width)
+            for e in range(2):
+                nc.vector.tensor_tensor(
+                    x[:, e, cols], pages[e][:].indirect(entries(read, j0, width)), wgt_sb[:, cols], ALU.mult
+                )
+            nc.vector.tensor_tensor(
+                z_bf[1][c][:, :, 2:4],
+                x[:, :, cols].rearrange("p e j -> p j e"),
+                tempo_sb[1][:, 2:4, cols].rearrange("p e j -> p j e"),
+                ALU.subtract,
+            )
+            zq = quantize(z_bf[1][c][:].rearrange("p j i -> p (j i)"), "z1q_%d" % c)
+            w5_passes(1, c)
+            w4_passes(1, c, zq, 0)
+            staged = ring.tile([P, N // P, width], F32, name="staged", tag="staged", bufs=3)
+            for nt in range(N // P):
+                nc.scalar.activation(staged[:, nt, :], acc(c, nt)[0], ACT.Identity, bias=b2_sb[:, nt : nt + 1])
+            nc.sync.dma_start(out_v[:, :, cols], staged[:])

@@ -156,33 +156,34 @@ def tile_list_fencing_bout_replay_kernel(
 
         h = [keep.tile([P, PACK, S], F32, name="h%d" % b) for b in range(2)]
 
-        def make_h(s):
+        def make_h(s, pieces):
             b, i = divmod(s, PACK)
-            for half in range(2):
-                bank = banks[2 * (s % 2) + half]
-                cols = slice(HALF * half, HALF * (half + 1))
+            for j0, width, bank in pieces:
+                cols = slice(j0, j0 + width)
                 for a in range(2):
                     codes, plane = w1q[a, b]
                     nc.tensor.matmul_mx(
-                        out=bank[:],
+                        out=bank[:, :width],
                         lhsT=codes[:, P * i : P * (i + 1)].bitcast(FP8X4),
                         lhsT_scale=plane[:, P * i : P * (i + 1)],
-                        rhs=picked[a, half][:].bitcast(FP8X4),
+                        rhs=picked[a, j0 // HALF][:, j0 % HALF : j0 % HALF + width].bitcast(FP8X4),
                         rhs_scale=picked_plane[4 * a : P, cols],
                         start=(a == 0),
                         stop=(a == 1),
                     )
-                nc.scalar.activation(h[b][:, i, cols], bank[:], ACT.Tanh, bias=b1_sb[:, b, i : i + 1])
+                nc.scalar.activation(h[b][:, i, cols], bank[:, :width], ACT.Tanh, bias=b1_sb[:, b, i : i + 1])
                 nc.scalar.activation(h[b][:, i, cols], h[b][:, i, cols], ACT.Copy, scale=gain_sb[:, b, i : i + 1])
 
-        def place(s, pieces):
+        def place(s, j0, width):
             b, i = divmod(s, PACK)
-            width = S // pieces
-            for n in range(pieces):
-                cols = slice(width * n, width * (n + 1))
-                nc.vector.tensor_tensor(
-                    pages[s % 2][:].indirect(entries(put, width * n, width)), h[b][:, i, cols], wgs_sb[:, cols], ALU.mult
-                )
+            cols = slice(j0, j0 + width)
+            nc.vector.tensor_tensor(
+                pages[s % 2][:].indirect(entries(put, j0, width)), h[b][:, i, cols], wgs_sb[:, cols], ALU.mult
+            )
+
+        def make_and_place(s):
+            make_h(s, [(HALF * half, HALF, banks[2 * (s % 2) + half]) for half in range(2)])
+            place(s, 0, S)
 
         neg_x = {}
 
@@ -196,71 +197,80 @@ def tile_list_fencing_bout_replay_kernel(
             [keep.tile([P, HALF, PACK], BF16, name="z0_%d" % n, align_bytes=64) for n in range(2)],
             [keep.tile([P, width, PACK], BF16, name="z1_%d" % j0, align_bytes=64) for j0, width in CHUNKS],
         ]
-        z_cols = [[(0, HALF), (HALF, HALF)], CHUNKS
-        ]
 
         def subtract_on_tensor(pair):
             b, u = divmod(pair, 2)
-            for half in range(2):
-                back = banks[6 + half]
-                for g in range(2):
-                    bank = banks[4 + g]
-                    steps = [(src, jb, e) for src in range(2) for jb in range(2) for e in range(2)]
-                    for n, (src, jb, e) in enumerate(steps):
-                        j0 = HALF * half + P * (2 * g + jb)
-                        rows = tempo_sb[b][:, 2 * u + e, j0 : j0 + P] if src == 0 else neg_x[pair][:, e, j0 : j0 + P]
-                        nc.tensor.matmul(
-                            bank[:, P * (2 * jb + e) : P * (2 * jb + e + 1)],
-                            lhsT=rows,
-                            rhs=ident[:],
-                            is_transpose=True,
-                            start=(n == 0),
-                            stop=(n == len(steps) - 1),
-                        )
-                    z_t = ring.tile([P, 2, P, 2], BF16, name="z_t", tag="z_t", bufs=4)
-                    nc.scalar.activation(
-                        z_t[:], bank[:].rearrange("j (jb e p) -> j jb p e", jb=2, e=2), ACT.Copy, scale=-1.0
+            turned = []
+            for g in range(4):
+                bank = banks[4 + g % 3]
+                steps = [(src, jb, e) for src in range(2) for jb in range(2) for e in range(2)]
+                for n, (src, jb, e) in enumerate(steps):
+                    j0 = P * (2 * g + jb)
+                    rows = tempo_sb[b][:, 2 * u + e, j0 : j0 + P] if src == 0 else neg_x[pair][:, e, j0 : j0 + P]
+                    nc.tensor.matmul(
+                        bank[:, P * (2 * jb + e) : P * (2 * jb + e + 1)],
+                        lhsT=rows,
+                        rhs=ident[:],
+                        is_transpose=True,
+                        start=(n == 0),
+                        stop=(n == len(steps) - 1),
                     )
-                    words = z_t[:].rearrange("j jb p e -> j jb (p e)").bitcast(F32)
+                z_t = ring.tile([P, 2, P, 2], BF16, name="z_t", tag="z_t", bufs=8)
+                nc.scalar.activation(
+                    z_t[:], bank[:].rearrange("j (jb e p) -> j jb p e", jb=2, e=2), ACT.Copy, scale=-1.0
+                )
+                turned.append(z_t[:].rearrange("j jb p e -> j jb (p e)").bitcast(F32))
+            return turned
+
+        def turn_back_both(low, high):
+            for g in range(4):
+                bank = banks[(7, 5, 6, 4)[g]]
+                for u, turned in enumerate((low, high)):
                     for jb in range(2):
-                        nc.tensor.transpose(back[:, P * (2 * g + jb) : P * (2 * g + jb + 1)], words[:, jb, :], ident[:])
-                for tile, (j0, width) in zip(z_bf[b], z_cols[b]):
+                        nc.tensor.transpose(bank[:, P * (2 * u + jb) : P * (2 * u + jb + 1)], turned[g][:, jb, :], ident[:])
+                dst = z_bf[0][g // 2][:, 256 * (g % 2) : 256 * (g % 2 + 1), :].bitcast(F32)
+                nc.scalar.copy(dst, bank[:].rearrange("p (u j) -> p j u", u=2))
+
+        def turn_back_low(low):
+            for half in range(2):
+                bank = banks[(7, 5)[half]]
+                for jb in range(4):
+                    nc.tensor.transpose(bank[:, P * jb : P * (jb + 1)], low[2 * half + jb // 2][:, jb % 2, :], ident[:])
+                for tile, (j0, width) in zip(z_bf[1], CHUNKS):
                     if j0 // HALF == half:
-                        nc.scalar.copy(tile[:].bitcast(F32)[:, :, u], back[:, j0 % HALF : j0 % HALF + width])
+                        nc.scalar.copy(tile[:].bitcast(F32)[:, :, 0], bank[:, j0 % HALF : j0 % HALF + width])
 
         def quantize_h(b):
             return [quantize_rows(h[b][:, :, HALF * n : HALF * (n + 1)], "h_bf", "h%d_%d" % (b, n)) for n in range(2)]
 
-        make_h(0)
-        place(0, 2)
-        make_h(1)
-        place(1, 1)
+        first_pieces = [(0, 256, banks[0]), (256, 256, banks[4]), (HALF, HALF, banks[1])]
+        for piece in first_pieces:
+            make_h(0, [piece])
+            place(0, piece[0], piece[1])
+        make_and_place(1)
         neg_wgt = keep.tile([P, S], F32, name="neg_wgt")
         nc.scalar.activation(neg_wgt[:], wgt_sb[:], ACT.Copy, scale=-1.0)
         fetch_negated(0)
         fetch_negated(1)
         w1q[0, 1] = quantize_w1(0, 1)
         w1q[1, 1] = quantize_w1(1, 1)
-        for s in (2, 3):
-            make_h(s)
-            place(s, 1)
-        subtract_on_tensor(0)
+        make_and_place(2)
+        make_and_place(3)
+        hq = [quantize_h(0)]
+        low = subtract_on_tensor(0)
         fetch_negated(2)
         fetch_negated(3)
-        hq = [quantize_h(0)]
-        for s in (4, 5):
-            make_h(s)
-            place(s, 1)
+        make_and_place(4)
+        make_and_place(5)
         w5q = [quantize_rows(w5_raw[a][:], "w_bf", "w5_%d" % a) for a in range(2)]
-        subtract_on_tensor(1)
+        turn_back_both(low, subtract_on_tensor(1))
         fetch_negated(4)
         fetch_negated(5)
         zq0 = [quantize(z_bf[0][n][:].rearrange("p j i -> p (j i)"), "z0q_%d" % n) for n in range(2)]
-        for s in (6, 7):
-            make_h(s)
-            place(s, 1)
+        make_and_place(6)
+        make_and_place(7)
         hq.append(quantize_h(1))
-        subtract_on_tensor(2)
+        turn_back_low(subtract_on_tensor(2))
 
         first_bank = [sum(width for j0, width in CHUNKS[:c]) * (N // P) // 512 for c in range(len(CHUNKS))]
 
@@ -324,6 +334,14 @@ def tile_list_fencing_bout_replay_kernel(
             w5_passes(1, c)
             w4_passes(1, c, zq, 0)
             staged = ring.tile([P, N // P, width], F32, name="staged", tag="staged", bufs=3)
-            for nt in range(N // P):
-                nc.scalar.activation(staged[:, nt, :], acc(c, nt)[0], ACT.Identity, bias=b2_sb[:, nt : nt + 1])
+            if c == len(CHUNKS) - 1:
+                nc.vector.tensor_tensor(
+                    staged[:],
+                    banks[first_bank[c]][:].rearrange("p (t j) -> p t j", j=width),
+                    b2_sb[:].unsqueeze(2).to_broadcast([P, N // P, width]),
+                    ALU.add,
+                )
+            else:
+                for nt in range(N // P):
+                    nc.scalar.activation(staged[:, nt, :], acc(c, nt)[0], ACT.Identity, bias=b2_sb[:, nt : nt + 1])
             nc.sync.dma_start(out_v[:, :, cols], staged[:])

@@ -32,6 +32,7 @@ def tile_list_fencing_bout_replay_kernel(
     with ExitStack() as ctx:
         keep = ctx.enter_context(tc.tile_pool(name="keep", bufs=1))
         ring = ctx.enter_context(tc.tile_pool(name="ring", bufs=2))
+        shared = ctx.enter_context(tc.tile_pool(name="shared", bufs=1))
         psum = ctx.enter_context(tc.psum_pool(name="psum", bufs=1))
 
         def entries(list_tile, start, count):
@@ -39,13 +40,16 @@ def tile_list_fencing_bout_replay_kernel(
 
         banks = [psum.tile([P, 512], F32, name="bank%d" % n) for n in range(8)]
 
-        pick = keep.tile([P, S // PER_COL], U16, name="pick")
-        nc.sync.dma_start(pick[:], offs)
+        table = [keep.tile([P, T], I32, name="table%d" % a, tag="slab%d" % a, align_bytes=64) for a in range(2)]
 
-        def load_table(a):
-            words = keep.tile([P, T], I32, name="table%d" % a, tag="slab%d" % a, align_bytes=64)
-            nc.sync.dma_start(words[:], tab_words[a].rearrange("p t i -> p (t i)").bitcast(I32))
-            return words
+        def load_table(a, start, stop):
+            src = tab_words[a].rearrange("p t i -> p (t i)").bitcast(I32)
+            nc.sync.dma_start(table[a][:, start:stop], src[:, start:stop])
+
+        def load_list(src, name):
+            tile = keep.tile([P, S // PER_COL], U16, name=name)
+            nc.sync.dma_start(tile[:], src)
+            return tile
 
         def load_weight(src, a, col0):
             raw = ring.tile([P, PACK, PASS], F32, name="raw", tag="raw", bufs=3)
@@ -54,32 +58,36 @@ def tile_list_fencing_bout_replay_kernel(
             )
             return raw
 
-        table_plane = keep.tile([P, T], U8, name="table_plane", align_bytes=64)
+        table_plane = shared.tile([P, T], U8, name="table_plane", align_bytes=64, offset=512)
         nc.vector.memset(table_plane[:].bitcast(I32), 0)
-        table = [load_table(0)]
 
-        def load_table_scales(a):
-            for r in range(4):
+        def load_table_scales(rows):
+            for a, r in rows:
                 nc.sync.dma_start(
                     table_plane[4 * a + r : P : 32, :].bitcast(I32), tab_scales[a, r:16:4, :].bitcast(I32)
                 )
 
-        load_table_scales(0)
+        scale_rows = [(a, r) for r in range(4) for a in range(2)]
+        load_table(0, 0, 1024)
+        pick = load_list(offs, "pick")
+        put = load_list(offs2, "put")
+        read = load_list(offs3, "read")
+        for start in range(1024, T, 768):
+            load_table(0, start, start + 768)
         w1_raw = {}
+        load_table_scales(scale_rows[:3])
         w1_raw[0, 0] = load_weight(w1, 0, 0)
+        load_table_scales(scale_rows[3:5])
         w1_raw[1, 0] = load_weight(w1, 1, 0)
-        load_table_scales(1)
-        table.append(load_table(1))
+        load_table_scales(scale_rows[5:])
+        load_table(1, 0, T)
         b1_sb = keep.tile([P, 2, PACK], F32, name="b1_sb")
         nc.sync.dma_start(b1_sb[:], b1.rearrange("(b p i) -> p b i", b=2, i=PACK))
         gain_sb = keep.tile([P, 2, PACK], F32, name="gain_sb")
         nc.sync.dma_start(gain_sb[:], gain.rearrange("(b p i) -> p b i", b=2, i=PACK))
-        put = keep.tile([P, S // PER_COL], U16, name="put")
-        nc.sync.dma_start(put[:], offs2)
         wgs_sb = keep.tile([P, S], F32, name="wgs_sb")
-        nc.sync.dma_start(wgs_sb[:], wgs)
-        read = keep.tile([P, S // PER_COL], U16, name="read")
-        nc.sync.dma_start(read[:], offs3)
+        nc.sync.dma_start(wgs_sb[:, :256], wgs[:, :256])
+        nc.sync.dma_start(wgs_sb[:, 256:], wgs[:, 256:])
         wgt_sb = keep.tile([P, S], F32, name="wgt_sb")
         nc.sync.dma_start(wgt_sb[:], wgt)
 
@@ -94,7 +102,10 @@ def tile_list_fencing_bout_replay_kernel(
         def quantize(grouped, name):
             width = grouped.shape[1] // PACK
             codes = keep.tile([P, width], U32, name=name + "_codes", align_bytes=64)
-            plane = keep.tile([P, width], U8, name=name + "_plane", align_bytes=64)
+            if name == "w1_10":
+                plane = shared.tile([P, width], U8, name=name + "_plane", align_bytes=64, offset=2048)
+            else:
+                plane = keep.tile([P, width], U8, name=name + "_plane", align_bytes=64)
             nc.vector.quantize_mx(out=codes[:].bitcast(FP8X4), scales=plane[:], in_=grouped)
             return codes, plane
 
@@ -117,7 +128,10 @@ def tile_list_fencing_bout_replay_kernel(
         picked = {}
 
         def pick_words(a, half):
-            tile = keep.tile([P, HALF], U32, name="picked%d%d" % (a, half), align_bytes=64)
+            if a == 0:
+                tile = keep.tile([P, HALF], U32, name="picked0%d" % half, align_bytes=64)
+            else:
+                tile = shared.tile([P, HALF], U32, name="picked1%d" % half, align_bytes=64, offset=2560 * half)
             nc.vector.tensor_copy(tile[:], table[a][:].bitcast(U32).indirect(entries(pick, HALF * half, HALF)))
             picked[a, half] = tile
 

from contextlib import ExitStack

import concourse.mybir as mybir
from concourse.masks import make_identity

K, H, N, T, S, T2 = 1024, 1024, 512, 4096, 1024, 2048
FLOPS = 2 * K * H * S + 2 * 2 * H * N * S

F32 = mybir.dt.float32
BF16 = mybir.dt.bfloat16
I32 = mybir.dt.int32
U32 = mybir.dt.uint32
U16 = mybir.dt.uint16
U8 = mybir.dt.uint8
FP8X4 = mybir.dt.float8_e4m3fn_x4
FP4X4 = mybir.dt.float4_e2m1fn_x4
ALU = mybir.AluOpType
ACT = mybir.ActivationFunctionType

P = 128
PACK = 4
PASS = P * PACK
HALF = 512
CHUNKS = [(0, 256), (256, 256), (512, 256), (768, 128), (896, 128)]
PER_COL = 16


def tile_list_fencing_bout_replay_kernel(
    tc, tab_words, tab_scales, offs, offs2, offs3, w1, b1, gain, wgs, wgt, tempo, w4_words, w4_scales, w5, b2, out
):
    nc = tc.nc
    with ExitStack() as ctx:
        keep = ctx.enter_context(tc.tile_pool(name="keep", bufs=1))
        ring = ctx.enter_context(tc.tile_pool(name="ring", bufs=2))
        shared = ctx.enter_context(tc.tile_pool(name="shared", bufs=1))
        psum = ctx.enter_context(tc.psum_pool(name="psum", bufs=1))

        def entries(list_tile, start, count):
            return list_tile[:, start // PER_COL : (start + count) // PER_COL]

        banks = [psum.tile([P, 512], F32, name="bank%d" % n) for n in range(8)]

        table = [keep.tile([P, T], I32, name="table%d" % a, tag="slab%d" % a, align_bytes=64) for a in range(2)]

        def load_table(a, start, stop):
            src = tab_words[a].rearrange("p t i -> p (t i)").bitcast(I32)
            nc.sync.dma_start(table[a][:, start:stop], src[:, start:stop])

        def load_list(src, name):
            tile = keep.tile([P, S // PER_COL], U16, name=name)
            nc.sync.dma_start(tile[:], src)
            return tile

        def load_weight(src, a, col0):
            raw = ring.tile([P, PACK, PASS], F32, name="raw", tag="raw", bufs=3)
            nc.sync.dma_start(
                raw[:], src[PASS * a : PASS * (a + 1), col0 : col0 + PASS].rearrange("(p j) c -> p j c", j=PACK)
            )
            return raw

        table_plane = shared.tile([P, T], U8, name="table_plane", align_bytes=64, offset=512)
        nc.vector.memset(table_plane[:].bitcast(I32), 0)

        def load_table_scales(rows):
            for a, r in rows:
                nc.sync.dma_start(
                    table_plane[4 * a + r : P : 32, :].bitcast(I32), tab_scales[a, r:16:4, :].bitcast(I32)
                )

        scale_rows = [(a, r) for r in range(4) for a in range(2)]
        load_table(0, 0, 1024)
        pick = load_list(offs, "pick")
        put = load_list(offs2, "put")
        read = load_list(offs3, "read")
        for start in range(1024, T, 768):
            load_table(0, start, start + 768)
        w1_raw = {}
        load_table_scales(scale_rows[:3])
        w1_raw[0, 0] = load_weight(w1, 0, 0)
        load_table_scales(scale_rows[3:5])
        w1_raw[1, 0] = load_weight(w1, 1, 0)
        load_table_scales(scale_rows[5:])
        load_table(1, 0, T)
        b1_sb = keep.tile([P, 2, PACK], F32, name="b1_sb")
        nc.sync.dma_start(b1_sb[:], b1.rearrange("(b p i) -> p b i", b=2, i=PACK))
        gain_sb = keep.tile([P, 2, PACK], F32, name="gain_sb")
        nc.sync.dma_start(gain_sb[:], gain.rearrange("(b p i) -> p b i", b=2, i=PACK))
        wgs_sb = keep.tile([P, S], F32, name="wgs_sb")
        nc.sync.dma_start(wgs_sb[:, :256], wgs[:, :256])
        nc.sync.dma_start(wgs_sb[:, 256:], wgs[:, 256:])
        wgt_sb = keep.tile([P, S], F32, name="wgt_sb")
        nc.sync.dma_start(wgt_sb[:], wgt)

        pages = [keep.tile([P, T2], F32, name="page%d" % n) for n in range(2)]
        for page in pages:
            nc.vector.memset(page[:], 0.0)
        w4_plane = keep.tile([P, 2, N], U8, name="w4_plane", align_bytes=64)
        nc.vector.memset(w4_plane[:].rearrange("p a n -> p (a n)").bitcast(I32), 0)
        ident = keep.tile([P, P], F32, name="ident")
        make_identity(nc, ident[:])

        def quantize(grouped, name):
            width = grouped.shape[1] // PACK
            codes = keep.tile([P, width], U32, name=name + "_codes", align_bytes=64)
            if name == "w1_10":
                plane = shared.tile([P, width], U8, name=name + "_plane", align_bytes=64, offset=2048)
            else:
                plane = keep.tile([P, width], U8, name=name + "_plane", align_bytes=64)
            nc.vector.quantize_mx(out=codes[:].bitcast(FP8X4), scales=plane[:], in_=grouped)
            return codes, plane

        def quantize_w1(a, b):
            grouped = ring.tile([P, PASS * PACK], BF16, name="w_bf", tag="w_bf", align_bytes=64)
            nc.scalar.copy(
                grouped[:].rearrange("p (t m j) -> p m t j", t=PACK, j=PACK),
                w1_raw[a, b][:].rearrange("p j (m t) -> p m t j", t=PACK),
            )
            return quantize(grouped[:], "w1_%d%d" % (a, b))

        def quantize_rows(src, tag, name):
            grouped = ring.tile([P, HALF * PACK], BF16, name=tag, tag=tag, align_bytes=64)
            nc.scalar.copy(
                grouped[:].rearrange("p (c i j) -> p c j i", i=4, j=PACK),
                src.rearrange("p j (c i) -> p c j i", i=4),
            )
            return quantize(grouped[:], name)

        picked = {}

        def pick_words(a, half):
            if a == 0:
                tile = keep.tile([P, HALF], U32, name="picked0%d" % half, align_bytes=64)
            else:
                tile = shared.tile([P, HALF], U32, name="picked1%d" % half, align_bytes=64, offset=2560 * half)
            nc.vector.tensor_copy(tile[:], table[a][:].bitcast(U32).indirect(entries(pick, HALF * half, HALF)))
            picked[a, half] = tile

        pick_words(0, 0)
        pick_words(0, 1)
        picked_plane = keep.tile([P, S], U8, name="picked_plane", align_bytes=64)
        nc.vector.tensor_copy(picked_plane[:], table_plane[:].indirect(pick[:]))
        w1q = {}
        w1q[0, 0] = quantize_w1(0, 0)
        w1q[1, 0] = quantize_w1(1, 0)
        pick_words(1, 0)
        pick_words(1, 1)

        w1_raw[0, 1] = load_weight(w1, 0, PASS)
        w1_raw[1, 1] = load_weight(w1, 1, PASS)

        def load_tempo(b):
            tile = keep.tile([P, PACK, S], F32, name="tempo%d" % b, tag="slab%d" % b, align_bytes=64)
            nc.sync.dma_start(tile[:], tempo[PASS * b : PASS * (b + 1), :].rearrange("(p i) j -> p i j", i=PACK))
            return tile

        tempo_sb = [load_tempo(0)]
        w5_raw = [load_weight(w5, a, 0) for a in range(2)]
        w4_sb = keep.tile([P, 2, 2 * N], U8, name="w4_sb", align_bytes=64)
        nc.sync.dma_start(
            w4_sb[:].bitcast(I32), w4_words.rearrange("a p c -> p a c").bitcast(I32)
        )
        for r in range(4):
            nc.sync.dma_start(
                w4_plane[r:P:32, :, :].bitcast(I32), w4_scales[:, r:16:4, :].rearrange("a q c -> q a c").bitcast(I32)
            )
        tempo_sb.append(load_tempo(1))
        b2_sb = keep.tile([P, N // P], F32, name="b2_sb")
        with nc.allow_non_contiguous_dma(reason="one bias value a partition"):
            nc.sync.dma_start(b2_sb[:], b2.rearrange("(t p) -> p t", p=P))

        h = [keep.tile([P, PACK, S], F32, name="h%d" % b) for b in range(2)]

        def make_h(s, pieces):
            b, i = divmod(s, PACK)
            for j0, width, bank in pieces:
                cols = slice(j0, j0 + width)
                for a in range(2):
                    codes, plane = w1q[a, b]
                    nc.tensor.matmul_mx(
                        out=bank[:, :width],
                        lhsT=codes[:, P * i : P * (i + 1)].bitcast(FP8X4),
                        lhsT_scale=plane[:, P * i : P * (i + 1)],
                        rhs=picked[a, j0 // HALF][:, j0 % HALF : j0 % HALF + width].bitcast(FP8X4),
                        rhs_scale=picked_plane[4 * a : P, cols],
                        start=(a == 0),
                        stop=(a == 1),
                    )
                nc.scalar.activation(h[b][:, i, cols], bank[:, :width], ACT.Tanh, bias=b1_sb[:, b, i : i + 1])
                nc.scalar.activation(h[b][:, i, cols], h[b][:, i, cols], ACT.Copy, scale=gain_sb[:, b, i : i + 1])

        def place(s, j0, width):
            b, i = divmod(s, PACK)
            cols = slice(j0, j0 + width)
            nc.vector.tensor_tensor(
                pages[s % 2][:].indirect(entries(put, j0, width)), h[b][:, i, cols], wgs_sb[:, cols], ALU.mult
            )

        def make_and_place(s):
            make_h(s, [(HALF * half, HALF, banks[2 * (s % 2) + half]) for half in range(2)])
            place(s, 0, S)

        neg_x = {}

        def fetch_negated(s):
            pair, e = divmod(s, 2)
            if e == 0:
                neg_x[pair] = ring.tile([P, 2, S], F32, name="neg_x", tag="x", bufs=1)
            nc.vector.tensor_tensor(neg_x[pair][:, e, :], pages[s % 2][:].indirect(read[:]), neg_wgt[:], ALU.mult)

        z_bf = [
            [keep.tile([P, HALF, PACK], BF16, name="z0_%d" % n, align_bytes=64) for n in range(2)],
            [keep.tile([P, width, PACK], BF16, name="z1_%d" % j0, align_bytes=64) for j0, width in CHUNKS],
        ]

        def subtract_on_tensor(pair):
            b, u = divmod(pair, 2)
            turned = []
            for g in range(4):
                bank = banks[4 + g % 3]
                steps = [(src, jb, e) for src in range(2) for jb in range(2) for e in range(2)]
                for n, (src, jb, e) in enumerate(steps):
                    j0 = P * (2 * g + jb)
                    rows = tempo_sb[b][:, 2 * u + e, j0 : j0 + P] if src == 0 else neg_x[pair][:, e, j0 : j0 + P]
                    nc.tensor.matmul(
                        bank[:, P * (2 * jb + e) : P * (2 * jb + e + 1)],
                        lhsT=rows,
                        rhs=ident[:],
                        is_transpose=True,
                        start=(n == 0),
                        stop=(n == len(steps) - 1),
                    )
                z_t = ring.tile([P, 2, P, 2], BF16, name="z_t", tag="z_t", bufs=8)
                nc.scalar.activation(
                    z_t[:], bank[:].rearrange("j (jb e p) -> j jb p e", jb=2, e=2), ACT.Copy, scale=-1.0
                )
                turned.append(z_t[:].rearrange("j jb p e -> j jb (p e)").bitcast(F32))
            return turned

        def turn_back_both(low, high):
            for g in range(4):
                bank = banks[(7, 5, 6, 4)[g]]
                for u, turned in enumerate((low, high)):
                    for jb in range(2):
                        nc.tensor.transpose(bank[:, P * (2 * u + jb) : P * (2 * u + jb + 1)], turned[g][:, jb, :], ident[:])
                dst = z_bf[0][g // 2][:, 256 * (g % 2) : 256 * (g % 2 + 1), :].bitcast(F32)
                nc.scalar.copy(dst, bank[:].rearrange("p (u j) -> p j u", u=2))

        def turn_back_low(low):
            for half in range(2):
                bank = banks[(7, 5)[half]]
                for jb in range(4):
                    nc.tensor.transpose(bank[:, P * jb : P * (jb + 1)], low[2 * half + jb // 2][:, jb % 2, :], ident[:])
                for tile, (j0, width) in zip(z_bf[1], CHUNKS):
                    if j0 // HALF == half:
                        nc.scalar.copy(tile[:].bitcast(F32)[:, :, 0], bank[:, j0 % HALF : j0 % HALF + width])

        def quantize_h(b):
            return [quantize_rows(h[b][:, :, HALF * n : HALF * (n + 1)], "h_bf", "h%d_%d" % (b, n)) for n in range(2)]

        first_pieces = [(0, 256, banks[0]), (256, 256, banks[4]), (HALF, HALF, banks[1])]
        for piece in first_pieces:
            make_h(0, [piece])
            place(0, piece[0], piece[1])
        make_and_place(1)
        neg_wgt = keep.tile([P, S], F32, name="neg_wgt")
        nc.scalar.activation(neg_wgt[:], wgt_sb[:], ACT.Copy, scale=-1.0)
        fetch_negated(0)
        fetch_negated(1)
        w1q[0, 1] = quantize_w1(0, 1)
        w1q[1, 1] = quantize_w1(1, 1)
        make_and_place(2)
        make_and_place(3)
        hq = [quantize_h(0)]
        low = subtract_on_tensor(0)
        fetch_negated(2)
        fetch_negated(3)
        make_and_place(4)
        make_and_place(5)
        w5q = [quantize_rows(w5_raw[a][:], "w_bf", "w5_%d" % a) for a in range(2)]
        turn_back_both(low, subtract_on_tensor(1))
        fetch_negated(4)
        fetch_negated(5)
        zq0 = [quantize(z_bf[0][n][:].rearrange("p j i -> p (j i)"), "z0q_%d" % n) for n in range(2)]
        make_and_place(6)
        make_and_place(7)
        hq.append(quantize_h(1))
        turn_back_low(subtract_on_tensor(2))

        first_bank = [sum(width for j0, width in CHUNKS[:c]) * (N // P) // 512 for c in range(len(CHUNKS))]

        def acc(c, nt):
            width = CHUNKS[c][1]
            bank, slot = divmod(nt, 512 // width)
            return banks[first_bank[c] + bank][:, width * slot : width * (slot + 1)], slot

        def w5_passes(b, c):
            j0, width = CHUNKS[c]
            codes, plane = hq[b][j0 // HALF]
            cols = slice(j0 % HALF, j0 % HALF + width)
            for nt in range(N // P):
                dst, slot = acc(c, nt)
                nc.tensor.matmul_mx(
                    out=dst,
                    lhsT=w5q[b][0][:, P * nt : P * (nt + 1)].bitcast(FP8X4),
                    lhsT_scale=w5q[b][1][:, P * nt : P * (nt + 1)],
                    rhs=codes[:, cols].bitcast(FP8X4),
                    rhs_scale=plane[:, cols],
                    start=(b == 0 and slot == 0),
                    stop=False,
                )

        def w4_passes(b, c, zq, col0):
            width = CHUNKS[c][1]
            codes, plane = zq
            for nt in range(N // P):
                dst, slot = acc(c, nt)
                for n in range(width // P):
                    cols = slice(col0 + P * n, col0 + P * (n + 1))
                    nc.tensor.matmul_mx(
                        out=dst[:, P * n : P * (n + 1)],
                        lhsT=w4_sb[:, b, 2 * P * nt : 2 * P * (nt + 1)].bitcast(FP4X4),
                        lhsT_scale=w4_plane[:, b, P * nt : P * (nt + 1)],
                        rhs=codes[:, cols].bitcast(FP8X4),
                        rhs_scale=plane[:, cols],
                        start=False,
                        stop=(b == 1 and slot == 512 // width - 1 and n == width // P - 1),
                    )

        for c, (j0, width) in enumerate(CHUNKS):
            w5_passes(0, c)
            w4_passes(0, c, zq0[j0 // HALF], j0 % HALF)

        out_v = out.rearrange("(t p) j -> p t j", p=P)
        x = ring.tile([P, 2, S], F32, name="x_tail", tag="x", bufs=1)
        for c, (j0, width) in enumerate(CHUNKS):
            cols = slice(j0, j0 + width)
            for e in range(2):
                nc.vector.tensor_tensor(
                    x[:, e, cols], pages[e][:].indirect(entries(read, j0, width)), wgt_sb[:, cols], ALU.mult
                )
            nc.vector.tensor_tensor(
                z_bf[1][c][:, :, 2:4],
                x[:, :, cols].rearrange("p e j -> p j e"),
                tempo_sb[1][:, 2:4, cols].rearrange("p e j -> p j e"),
                ALU.subtract,
            )
            zq = quantize(z_bf[1][c][:].rearrange("p j i -> p (j i)"), "z1q_%d" % c)
            w5_passes(1, c)
            w4_passes(1, c, zq, 0)
            staged = ring.tile([P, N // P, width], F32, name="staged", tag="staged", bufs=3)
            if c == len(CHUNKS) - 1:
                nc.vector.tensor_tensor(
                    staged[:],
                    banks[first_bank[c]][:].rearrange("p (t j) -> p t j", j=width),
                    b2_sb[:].unsqueeze(2).to_broadcast([P, N // P, width]),
                    ALU.add,
                )
            else:
                for nt in range(N // P):
                    nc.scalar.activation(staged[:, nt, :], acc(c, nt)[0], ACT.Identity, bias=b2_sb[:, nt : nt + 1])
            nc.sync.dma_start(out_v[:, :, cols], staged[:])
